import numpy as np, ml_dtypes
CORES = [44,45,46,47,172,173,174,175,300,301,302,303,428,429,430,431]
N = 16
import mx_ref
NC, G = 256, 2
C, C2 = np.float32(0.043), np.float32(0.041)
CNT = [[0,0,40,48,16,16,40,0,16,24,0,16,0,0,24,16],[64,0,24,8,8,16,8,40,0,24,24,8,16,0,16,0],[48,0,16,0,16,16,0,0,0,24,16,32,8,0,24,56],[24,0,16,16,0,0,24,40,24,0,0,48,8,16,16,24],[0,48,32,32,24,8,16,0,24,0,24,0,0,24,8,16],[0,16,0,48,16,0,16,8,24,8,16,8,48,24,0,24],[24,8,0,0,0,8,24,0,16,56,16,24,32,0,24,24],[16,8,8,0,8,32,16,56,0,72,8,0,24,8,0,0],[8,24,8,40,56,32,48,0,8,0,0,8,8,0,16,0],[0,8,0,0,24,72,0,8,16,8,40,40,8,32,0,0],[16,32,32,0,0,24,24,16,16,8,0,0,8,0,72,8],[0,8,0,8,80,0,8,16,24,0,0,16,16,32,24,24],[32,0,32,8,0,8,0,16,24,0,8,8,40,48,0,32],[0,24,0,24,0,0,0,16,0,0,56,16,40,40,24,16],[24,40,48,16,8,0,0,32,0,8,24,24,0,32,0,0],[0,40,0,8,0,24,32,8,64,24,24,8,0,0,8,16]]
OFF = [[sum(c[:e]) for e in range(N + 1)] for c in CNT]
BF = ml_dtypes.bfloat16
def cut(t, i, w=512):
    return t[:, w * i:w * i + w]
def tile(rs):
    return np.stack(rs, axis=2).reshape(128, -1).astype(BF)
def layer(w, X):
    out = []
    for i in range(G):
        for t in range(len(X)):
            p = mx_ref.matmul(mx_ref.quantize(cut(w, len(X) * i + t)), X[t])
            z = p if t == 0 else z + p
        out.append(z)
    return out
def act(Z):
    return [np.maximum(s * z, 0) * C for z in Z for s in (1, -1)]
def setup_inputs(rng):
    def f(*shape):
        return mx_ref.flush((rng.standard_normal(shape, dtype=np.float32) * np.exp2(rng.integers(-2, 3, shape[:-1] + (1,)))).astype(BF))
    return {"x": f(N, 128, 4 * NC), "w1": f(N, 128, G * 512), "w2": f(N, 128, G * 512), "w3": f(N, 128, 512)}
def setup_inputs_blocks(rng):
    d = setup_inputs(rng)
    for k in ("x", "w3"): d[k] = mx_ref.spread(d[k], rng, 4)
    for k in ("w1", "w2"): d[k] = mx_ref.spread(d[k], rng, 2)
    return d
def setup_inputs_wide(rng):
    d = setup_inputs(rng)
    for k in ("x", "w1", "w2", "w3"): d[k] = mx_ref.flush((d[k].astype(np.float32) * np.exp2(rng.integers(-4, 5, (N, 1, 1))).astype(np.float32)).astype(BF))
    return d
def setup_inputs_zeros(rng):
    d = setup_inputs(rng); v = d["x"].reshape(N, 128, -1, 4).copy()
    v[np.broadcast_to((rng.random((N, 1, v.shape[2], 1)) < 0.33), v.shape)] = 0
    d["x"] = v.reshape(d["x"].shape)
    return d
def act2(Z):
    return [np.maximum(s * z, 0) * C2 for z in Z for s in (1, -1)]
def reference(x, w1, w2, w3):
    h = [tile(act(layer(w1[j], [mx_ref.quantize(x[j])]))) for j in range(N)]
    g = []
    for e in range(N):
        t = np.concatenate([h[j][:, 4 * OFF[j][e]:4 * OFF[j][e + 1]] for j in range(N)], axis=1)
        g.append(tile(act2(layer(w2[e], [mx_ref.quantize(t)]))))
    y = np.zeros((N, 128, NC), np.float32)
    for j in range(N):
        back = []
        for e in range(N):
            a = sum(CNT[i][e] for i in range(j))
            back.append(g[e][:, 4 * a:4 * a + 4 * CNT[j][e]])
        y[j] = mx_ref.matmul(mx_ref.quantize(w3[j]), mx_ref.quantize(np.concatenate(back, axis=1)))
    return {"y": y}

@@ -1,0 +1,306 @@
+from concourse.bass import DstId, RemoteDMATransfer
+from concourse.mybir import dt, AluOpType, ActivationFunctionType
+
+NC = 256
+C1, C2 = 0.043, 0.041
+LEAST = 1280
+SIM_CORES = 512
+CABLE_TWIN = (0, 3, 4, 6, 8, 10, 13, 14)
+ALPHA = 45
+
+CODES, PLANE = "float8_e4m3fn_x4", "uint8"
+SCRATCH = {
+    "xt": ("sbuf", [128, 1024], "bfloat16"),
+    "w1t": ("sbuf", [128, 1024], "bfloat16"),
+    "w2t": ("sbuf", [128, 1024], "bfloat16"),
+    "w3t": ("sbuf", [128, 512], "bfloat16"),
+    "ht": ("sbuf", [128, 1024], "bfloat16"),
+    "gt": ("sbuf", [128, 2048], "bfloat16"),
+    "ysb": ("sbuf", [128, 256], "float32"),
+    "xq": ("sbuf", [128, 256], CODES), "xs": ("sbuf", [128, 256], PLANE),
+    "w1q": ("sbuf", [128, 256], CODES), "w1s": ("sbuf", [128, 256], PLANE),
+    "w2q": ("sbuf", [128, 256], CODES), "w2s": ("sbuf", [128, 256], PLANE),
+    "w3q": ("sbuf", [128, 128], CODES), "w3s": ("sbuf", [128, 128], PLANE),
+    "bq": ("sbuf", [128, 768], CODES), "bs": ("sbuf", [128, 768], PLANE),
+    "gq": ("sbuf", [128, 512], CODES), "gs": ("sbuf", [128, 512], PLANE),
+    "aq": ("sbuf", [128, 768], CODES), "as_": ("sbuf", [128, 768], PLANE),
+    "ps": ("psum", [128, 4096], "float32"),
+}
+SEMAPHORES = ["lx", "lw1", "lw2", "lw3", "qx", "qw1", "qw2", "qw3", "qh", "qg", "z0", "z1", "o0", "o1", "u0", "u1",
+              "av", "aw", "bv", "bw", "pad", "sent", "w2in", "tok", "ret", "yo", "y1", "y2", "cv", "cw", "st1", "st2"]
+_CACHE = {}
+
+
+def widths(counts):
+    ds = sorted(set(counts))
+    best = None
+    for m in range(1 << (len(ds) - 1)):
+        ws = [d for i, d in enumerate(ds[:-1]) if m >> i & 1] + [ds[-1]]
+        cost = 2 * ALPHA * len(ws) + sum(min(w for w in ws if w >= c) - c for c in counts)
+        if best is None or cost < best[0]:
+            best = (cost, ws)
+    return best[1]
+
+
+def make_plan(T, topo):
+    cnt, cores = T.tables["CNT"], list(T.cores)
+    n = len(cores)
+    off = [[sum(c[:e]) for e in range(n + 1)] for c in cnt]
+    host = [topo.host(c) for c in cores]
+    twin, used, role = {}, {}, {}
+    for cabled in (False, True):
+        for e in range(n):
+            if (e in CABLE_TWIN) != cabled:
+                continue
+            th = [h for h in sorted(set(host)) if h != host[e] and topo.may_write(cores[e], cores[host.index(h)])
+                  and (topo.rack(h) != topo.rack(host[e])) == cabled][0]
+            free = [c for c in range(SIM_CORES) if topo.host(c) == th and topo.chip(c) == topo.chip(cores[e]) and T.rank_of(c) is None]
+            k = used.get((th, cabled), 0)
+            used[(th, cabled)] = k + 1
+            twin[e] = free[2 * k + int(cabled)]
+            role[twin[e]] = e
+    def site(j, e):
+        if host[j] != topo.host(twin[e]) and topo.may_write(cores[j], cores[e]):
+            return cores[e]
+        return twin[e]
+    slots, land = {}, {}
+    outs = {}
+    for j in range(n):
+        items = [(e, cnt[j][e]) for e in range(n) if e != j and cnt[j][e]]
+        ws = widths([c for _, c in items])
+        for e, c in items:
+            w = min(v for v in ws if v >= c)
+            s = min(off[j][e], NC - w)
+            d = site(j, e)
+            p = land.get(d, 0)
+            land[d] = p + w
+            slots.setdefault(d, []).append((j, p, off[j][e] - s, c))
+            outs.setdefault(cores[j], []).append((d, s, NC + p, w))
+    back, pieces, gn = {}, {}, {}
+    for s in sorted(slots):
+        e = role[s] if s in role else T.rank_of(s)
+        own = cnt[e][e] if s not in role else 0
+        gn[s] = max(128, own + land[s])
+        ws = widths([c for _, _, _, c in slots[s]])
+        for j, p, o, c in slots[s]:
+            w = min(v for v in ws if v >= c)
+            col = own + p + o
+            src = min(col, gn[s] - w)
+            pieces.setdefault(j, []).append((e, s, w, col - src, c, src))
+    asl = {}
+    for j in range(n):
+        pos = 0
+        asl[j] = []
+        for e, s, w, o, c, src in sorted(pieces[j]):
+            asl[j].append((e, pos, o, c))
+            back.setdefault(s, []).append((cores[j], src, pos, w))
+            pos += w
+        asl[j].append((n, pos, 0, 0))
+    return {"cnt": cnt, "off": off, "twin": twin, "role": role, "land": land, "outs": outs, "back": back, "asl": asl, "gn": gn}
+
+
+def bits(mask):
+    return [b for b in range(16) if mask >> b & 1]
+
+
+def calls(core, runs, topo, load, ends):
+    out = []
+    outside = 0
+    for c in ends:
+        if topo.host(c) != topo.host(core) and topo.may_write(core, c):
+            outside = outside | topo.mask(core, c)
+    for w in sorted(set(r[3] for r in runs), reverse=True):
+        group = [r for r in runs if r[3] == w]
+        far = [r for r in group if topo.chip(r[0]) != topo.chip(core) or topo.host(r[0]) != topo.host(core)]
+        near = [r for r in group if r not in far]
+        for codes in (True, False):
+            call = []
+            for part in (far, near):
+                if not part:
+                    continue
+                pool = bits(outside) if part is far else [b for b in bits(topo.mask(core, part[0][0])) if not far or not outside >> b & 1]
+                p = 1
+                while 2 * p * len(part) <= len(pool):
+                    p *= 2
+                extra = (len(pool) - p * len(part)) // p
+                pool = sorted(pool, key=lambda b: (load[b], b))
+                for i, r in enumerate(part):
+                    k = p if i < len(part) - extra else 2 * p
+                    es, pool = pool[:k], pool[k:]
+                    call.append((r, sum(1 << b for b in es)))
+                    for b in es:
+                        load[b] += (40 + (4 * w if codes else w) / 12.0) / k
+            out.append((codes, call))
+    return out
+
+
+def send(g, T, topo, core, todo, q, s, dq, ds, sem):
+    total = 0
+    for codes, call in todo:
+        tr = []
+        for (d, a, b, w), mask in call:
+            rid, pid = topo.addr(d, core)
+            src = q[:, a:a + w].bitcast(dt.uint8) if codes else s[:, a:a + w]
+            dst = dq[:, b:b + w].bitcast(dt.uint8) if codes else ds[:, b:b + w]
+            tr.append(RemoteDMATransfer(dst_ids=[DstId(rid=rid, pnc=pid)], dma_engine_mask=mask, remote_sem=sem, src=src, dst=dst))
+            total += len(bits(mask))
+        g.remote_dma_fused(tr, local_sem=T.sem.sent)
+    return total
+
+
+def signs(g, T, which, bank, n0, n1, t0, c, tile, sem):
+    z = T.ps[:, 512 * bank + n0:512 * bank + n1]
+    e = t0 + n1 - n0
+    for k, sg in enumerate((1.0, -1.0)):
+        out = tile[:, 4 * t0 + 2 * which + k:4 * e:4]
+        if which == 0:
+            g.vector.tensor_scalar(out, z, sg * c, 0.0, AluOpType.mult, AluOpType.max).then_inc(sem, 1)
+        else:
+            g.scalar.activation(out, z, ActivationFunctionType.Relu, scale=sg * c).then_inc(sem, 1)
+
+
+def product(g, T, banks, wq, ws, q, s, b0, n, sems):
+    for i in (0, 1):
+        g.tensor.matmul_mx(T.ps[:, 512 * banks[i]:512 * banks[i] + n], wq[:, 128 * i:128 * i + 128], ws[:, 128 * i:128 * i + 128],
+                           q[:, b0:b0 + n], s[:, b0:b0 + n], True, True).then_inc(sems[i], 1)
+
+
+def rank_program(g, core, T, topo):
+    if "plan" not in _CACHE:
+        P = make_plan(T, topo)
+        P["todo"], P["rise"] = {}, {}
+        for c in sorted(set(P["outs"]) | set(P["back"])):
+            load = [0.0] * 16
+            for k in ("outs", "back"):
+                P["todo"][c, k] = calls(c, P[k].get(c, []), topo, load, T.cores)
+                for _, call in P["todo"][c, k]:
+                    for r, mask in call:
+                        P["rise"][r[0], k] = P["rise"].get((r[0], k), 0) + len(bits(mask))
+        _CACHE["plan"] = P
+    P = _CACHE["plan"]
+    rank = T.rank_of(core)
+    if rank is None and core not in P["role"]:
+        return
+    S = T.sem
+    a = P["land"][core]
+    tok = P["rise"][core, "outs"]
+    gn = P["gn"][core]
+    own = P["cnt"][rank][rank] if rank is not None else 0
+    sent = 0
+    padded = gn > own + a
+    if padded:
+        g.vector.memset(T.gt[:, 4 * (own + a):4 * gn], 0.0).then_inc(S.pad, 1)
+
+    def expert(wq, ws, nb, full):
+        g.tensor.wait_ge(S.tok, tok)
+        product(g, T, (4, 5), wq, ws, T.bq, T.bs, NC + a - nb, nb, (S.u0, S.u1))
+        g.vector.wait_ge(S.u0, 1)
+        signs(g, T, 0, 4, nb - a, nb, own, C2, T.gt, S.bv)
+        g.scalar.wait_ge(S.u1, 1)
+        signs(g, T, 1, 5, nb - a, nb, own, C2, T.gt, S.bw)
+        if padded:
+            g.vector.wait_ge(S.pad, 1)
+        g.vector.wait_ge(S.bv, full)
+        g.vector.wait_ge(S.bw, full)
+        g.vector.quantize_mx(T.gq[:, 0:gn], T.gs[:, 0:gn], T.gt[:, 0:4 * gn]).then_inc(S.qg, 1)
+        g.wait_ge(S.qg, 1)
+        k = send(g, T, topo, core, P["todo"][core, "back"], T.gq, T.gs, T.aq, T.as_, S.ret)
+        g.wait_ge(S.sent, sent + k)
+
+    if rank is None:
+        g.tensor.wait_ge(S.w2in, 2 * len(bits(topo.mask(T.cores[P["role"][core]], core))))
+        expert(T.bq, T.bs, max(128, a), 2)
+        return
+
+    off = P["off"][rank]
+    o0 = off[rank]
+    asl = P["asl"][rank]
+    ret = P["rise"][core, "back"]
+
+    g.sync.dma_start(T.xt[:], T.x[:]).then_inc(S.lx, 16)
+    g.scalar.dma_start(T.w1t[:], T.w1[:]).then_inc(S.lw1, 16)
+    g.sync.dma_start(T.w2t[:], T.w2[:]).then_inc(S.lw2, 16)
+    g.scalar.dma_start(T.w3t[:], T.w3[:]).then_inc(S.lw3, 16)
+
+    g.vector.wait_ge(S.lx, 16)
+    g.vector.quantize_mx(T.xq[:], T.xs[:], T.xt[:]).then_inc(S.qx, 1)
+    g.vector.wait_ge(S.lw1, 16)
+    g.vector.quantize_mx(T.w1q[:], T.w1s[:], T.w1t[:]).then_inc(S.qw1, 1)
+    g.tensor.wait_ge(S.qx, 1)
+    g.tensor.wait_ge(S.qw1, 1)
+    product(g, T, (0, 1), T.w1q, T.w1s, T.xq, T.xs, 0, NC, (S.z0, S.z1))
+    g.vector.wait_ge(S.z0, 1)
+    signs(g, T, 0, 0, 0, NC, 0, C1, T.ht, S.av)
+    g.scalar.wait_ge(S.z1, 1)
+    signs(g, T, 1, 1, 0, NC, 0, C1, T.ht, S.aw)
+    g.vector.wait_ge(S.lw2, 16)
+    g.vector.quantize_mx(T.w2q[:], T.w2s[:], T.w2t[:]).then_inc(S.qw2, 1)
+    g.vector.wait_ge(S.av, 2)
+    g.vector.wait_ge(S.aw, 2)
+    g.vector.quantize_mx(T.bq[:, 0:NC], T.bs[:, 0:NC], T.ht[:]).then_inc(S.qh, 1)
+
+    tw = P["twin"][rank]
+    rid, pid = topo.addr(tw, core)
+    m = topo.mask(core, tw)
+    g.wait_ge(S.qw2, 1)
+    g.remote_dma(T.bq[:, 0:NC].bitcast(dt.uint8), T.w2q[:].bitcast(dt.uint8), S.w2in, S.sent, pid, rid, m)
+    g.remote_dma(T.bs[:, 0:NC], T.w2s[:], S.w2in, S.sent, pid, rid, m)
+    sent += 2 * len(bits(m))
+    g.wait_ge(S.qh, 1)
+    sent += send(g, T, topo, core, P["todo"][core, "outs"], T.bq, T.bs, T.bq, T.bs, S.tok)
+
+    half = ((len(asl) - 1) * 3 + 2) // 5
+    e_split = asl[half][0]
+    n1, ntot = asl[half][1], asl[-1][1]
+    na1, na2 = max(128, n1), max(128, ntot - n1)
+    fixed = 2 * NC + (2 * 128 + 128 if own else 0) + na1 + na2
+    ow = min(o0, NC - 128)
+    g.tensor.wait_ge(S.qh, 1)
+    g.tensor.wait_ge(S.qw2, 1)
+    if own:
+        product(g, T, (2, 3), T.w2q, T.w2s, T.bq, T.bs, ow, 128, (S.o0, S.o1))
+        g.vector.wait_ge(S.o0, 1)
+        signs(g, T, 0, 2, o0 - ow, o0 - ow + own, 0, C2, T.gt, S.bv)
+        g.scalar.wait_ge(S.o1, 1)
+        signs(g, T, 1, 3, o0 - ow, o0 - ow + own, 0, C2, T.gt, S.bw)
+    g.vector.wait_ge(S.lw3, 16)
+    g.vector.quantize_mx(T.w3q[:], T.w3s[:], T.w3t[:]).then_inc(S.qw3, 1)
+
+    expert(T.w2q, T.w2s, max(128, a, (LEAST - fixed + 3) // 4 * 2), 4 if own else 2)
+
+    g.tensor.wait_ge(S.qw3, 1)
+    if own:
+        g.tensor.wait_ge(S.qg, 1)
+        g.tensor.matmul_mx(T.ps[:, 1024:1024 + 128], T.w3q[:], T.w3s[:], T.gq[:, 0:128], T.gs[:, 0:128], True, True).then_inc(S.yo, 1)
+    g.tensor.wait_ge(S.ret, ret)
+    g.tensor.matmul_mx(T.ps[:, 3072:3072 + na1], T.w3q[:], T.w3s[:], T.aq[:, 0:na1], T.as_[:, 0:na1], True, True).then_inc(S.y1, 1)
+    g.tensor.matmul_mx(T.ps[:, 3584:3584 + na2], T.w3q[:], T.w3s[:], T.aq[:, ntot - na2:ntot], T.as_[:, ntot - na2:ntot],
+                       True, True).then_inc(S.y2, 1)
+    for part in (0, 1):
+        eng, sem, done = (g.vector, S.y1, S.cv) if part == 0 else (g.scalar, S.y2, S.cw)
+        base = 3072 if part == 0 else 3584 - (ntot - na2)
+        segs = []
+        for e, pos, o, c in (asl[:half] if part == 0 else asl[half:-1]):
+            y0, src = off[e], base + pos + o
+            if segs and segs[-1][1] == y0 and segs[-1][2] + segs[-1][1] - segs[-1][0] == src:
+                segs[-1][1] = y0 + c
+            else:
+                segs.append([y0, y0 + c, src])
+        mine = own and (rank < e_split) == (part == 0)
+        if mine:
+            segs.insert(0, [o0, o0 + own, 1024])
+        for i, (lo, hi, src) in enumerate(segs):
+            if mine and i == 0:
+                eng.wait_ge(S.yo, 1)
+            if i == (1 if mine else 0):
+                eng.wait_ge(sem, 1)
+            if part == 0:
+                g.vector.tensor_copy(T.ysb[:, lo:hi], T.ps[:, src:src + hi - lo]).then_inc(done, 1)
+            else:
+                g.scalar.activation(T.ysb[:, lo:hi], T.ps[:, src:src + hi - lo], ActivationFunctionType.Copy).then_inc(done, 1)
+        q, st = (g.sync, S.st1) if part == 0 else (g.scalar, S.st2)
+        lo, hi = (0, off[e_split]) if part == 0 else (off[e_split], NC)
+        q.wait_ge(done, len(segs))
+        q.dma_start(T.y[:, lo:hi], T.ysb[:, lo:hi]).then_inc(st, 16)
+    g.sync.wait_ge(S.st1, 16)
+    g.scalar.wait_ge(S.st2, 16)

@@ -6,6 +6,7 @@ C1, C2 = 0.043, 0.041
 LEAST = 1280
 SIM_CORES = 512
 CABLE_TWIN = (0, 3, 4, 6, 8, 10, 13, 14)
+HW, FC = 128, 192
 ALPHA = 45
 
 CODES, PLANE = "float8_e4m3fn_x4", "uint8"
@@ -21,13 +22,15 @@ SCRATCH = {
     "w1q": ("sbuf", [128, 256], CODES), "w1s": ("sbuf", [128, 256], PLANE),
     "w2q": ("sbuf", [128, 256], CODES), "w2s": ("sbuf", [128, 256], PLANE),
     "w3q": ("sbuf", [128, 128], CODES), "w3s": ("sbuf", [128, 128], PLANE),
+    "fq": ("sbuf", [128, 256], CODES),
     "bq": ("sbuf", [128, 768], CODES), "bs": ("sbuf", [128, 768], PLANE),
     "gq": ("sbuf", [128, 512], CODES), "gs": ("sbuf", [128, 512], PLANE),
     "aq": ("sbuf", [128, 768], CODES), "as_": ("sbuf", [128, 768], PLANE),
     "ps": ("psum", [128, 4096], "float32"),
 }
-SEMAPHORES = ["lx", "lw1", "lw2", "lw3", "qx", "qw1", "qw2", "qw3", "qh", "qg", "z0", "z1", "o0", "o1", "u0", "u1",
-              "av", "aw", "bv", "bw", "pad", "sent", "w2in", "tok", "ret", "yo", "y1", "y2", "cv", "cw", "st1", "st2"]
+SEMAPHORES = ["lx", "lw1", "lw1b", "lw2", "lw2b", "lw3", "qx", "qw1", "qw1b", "qw2", "qw2b", "qw3", "qh", "qg", "qf",
+              "z0", "z1", "z2", "z3", "o0", "o1", "u0", "u1", "v0", "v1", "av", "aw", "bv", "bw", "fv", "fw", "pad", "sent",
+              "w2in", "fin", "tokn", "tokf", "ret", "yo", "y1", "y2", "cv", "cw", "st1", "st2"]
 _CACHE = {}
 
 
@@ -42,11 +45,19 @@ def widths(counts):
     return best[1]
 
 
+def on_chip(topo, a, b):
+    return topo.chip(a) == topo.chip(b) and topo.host(a) == topo.host(b)
+
+
 def make_plan(T, topo):
     cnt, cores = T.tables["CNT"], list(T.cores)
     n = len(cores)
     off = [[sum(c[:e]) for e in range(n + 1)] for c in cnt]
     host = [topo.host(c) for c in cores]
+
+    def spare(h, e):
+        return [c for c in range(SIM_CORES) if topo.host(c) == h and topo.chip(c) == topo.chip(cores[e]) and T.rank_of(c) is None]
+
     twin, used, role = {}, {}, {}
     for cabled in (False, True):
         for e in range(n):
@@ -54,17 +65,21 @@ def make_plan(T, topo):
                 continue
             th = [h for h in sorted(set(host)) if h != host[e] and topo.may_write(cores[e], cores[host.index(h)])
                   and (topo.rack(h) != topo.rack(host[e])) == cabled][0]
-            free = [c for c in range(SIM_CORES) if topo.host(c) == th and topo.chip(c) == topo.chip(cores[e]) and T.rank_of(c) is None]
             k = used.get((th, cabled), 0)
             used[(th, cabled)] = k + 1
-            twin[e] = free[2 * k + int(cabled)]
+            twin[e] = spare(th, e)[2 * k + int(cabled)]
             role[twin[e]] = e
+    fwd, fwdof = {}, {}
+    for e in range(n):
+        k = [f for f in range(n) if host[f] == host[e] and (f in CABLE_TWIN) == (e in CABLE_TWIN)].index(e)
+        fwd[e] = spare(host[e], e)[2 * k + int(e in CABLE_TWIN)]
+        fwdof[fwd[e]] = e
+
     def site(j, e):
         if host[j] != topo.host(twin[e]) and topo.may_write(cores[j], cores[e]):
             return cores[e]
         return twin[e]
-    slots, land = {}, {}
-    outs = {}
+    runs, outs = {}, {}
     for j in range(n):
         items = [(e, cnt[j][e]) for e in range(n) if e != j and cnt[j][e]]
         ws = widths([c for _, c in items])
@@ -72,21 +87,29 @@ def make_plan(T, topo):
             w = min(v for v in ws if v >= c)
             s = min(off[j][e], NC - w)
             d = site(j, e)
-            p = land.get(d, 0)
-            land[d] = p + w
-            slots.setdefault(d, []).append((j, p, off[j][e] - s, c))
-            outs.setdefault(cores[j], []).append((d, s, NC + p, w))
-    back, pieces, gn = {}, {}, {}
-    for s in sorted(slots):
-        e = role[s] if s in role else T.rank_of(s)
-        own = cnt[e][e] if s not in role else 0
-        gn[s] = max(128, own + land[s])
-        ws = widths([c for _, _, _, c in slots[s]])
-        for j, p, o, c in slots[s]:
-            w = min(v for v in ws if v >= c)
-            col = own + p + o
-            src = min(col, gn[s] - w)
-            pieces.setdefault(j, []).append((e, s, w, col - src, c, src))
+            runs.setdefault(d, {True: [], False: []})[on_chip(topo, cores[j], d)].append((j, w, s, off[j][e] - s, c))
+    back, pieces, group = {}, {}, {}
+    for d in sorted(runs):
+        e = role[d] if d in role else T.rank_of(d)
+        p, t0 = 0, 0
+        group[d] = []
+        for near in (True, False):
+            own = cnt[e][e] if d not in role and near else 0
+            p0 = p
+            ws = widths([r[4] for r in runs[d][near]]) if runs[d][near] else []
+            tn = max(128, own + sum(r[1] for r in runs[d][near]))
+            for j, w, s, o, c in runs[d][near]:
+                outs.setdefault(cores[j], []).append((d, s, NC + p, w))
+                v = min(v for v in ws if v >= c)
+                col = own + p - p0 + o
+                src = min(col, tn - v)
+                pieces.setdefault(j, []).append((e, d, v, col - src, c, t0 + src))
+                p += w
+            if own or p > p0:
+                group[d].append((near, own, p0, p, t0, tn))
+                t0 += tn
+    for c in outs:
+        outs[c].sort(key=lambda r: r[1])
     asl = {}
     for j in range(n):
         pos = 0
@@ -96,7 +119,8 @@ def make_plan(T, topo):
             back.setdefault(s, []).append((cores[j], src, pos, w))
             pos += w
         asl[j].append((n, pos, 0, 0))
-    return {"cnt": cnt, "off": off, "twin": twin, "role": role, "land": land, "outs": outs, "back": back, "asl": asl, "gn": gn}
+    return {"cnt": cnt, "off": off, "twin": twin, "role": role, "outs": outs, "back": back, "asl": asl, "group": group,
+            "fwd": fwd, "fwdof": fwdof}
 
 
 def bits(mask):
@@ -111,7 +135,7 @@ def calls(core, runs, topo, load, ends):
             outside = outside | topo.mask(core, c)
     for w in sorted(set(r[3] for r in runs), reverse=True):
         group = [r for r in runs if r[3] == w]
-        far = [r for r in group if topo.chip(r[0]) != topo.chip(core) or topo.host(r[0]) != topo.host(core)]
+        far = [r for r in group if not on_chip(topo, r[0], core)]
         near = [r for r in group if r not in far]
         for codes in (True, False):
             call = []
@@ -134,15 +158,27 @@ def calls(core, runs, topo, load, ends):
     return out
 
 
-def send(g, T, topo, core, todo, q, s, dq, ds, sem):
+def near_mask(topo, T, e, c):
+    out = 0
+    for t in T.cores:
+        if topo.host(t) != topo.host(T.cores[e]) and topo.may_write(T.cores[e], t):
+            out = out | topo.mask(T.cores[e], t)
+    return topo.mask(T.cores[e], c) & ~out
+
+
+def transfer(topo, core, dst, mask, sem, src, to):
+    rid, pid = topo.addr(dst, core)
+    return RemoteDMATransfer(dst_ids=[DstId(rid=rid, pnc=pid)], dma_engine_mask=mask, remote_sem=sem, src=src, dst=to)
+
+
+def send(g, T, topo, core, todo, q, s, dq, ds, sems):
     total = 0
     for codes, call in todo:
         tr = []
         for (d, a, b, w), mask in call:
-            rid, pid = topo.addr(d, core)
             src = q[:, a:a + w].bitcast(dt.uint8) if codes else s[:, a:a + w]
             dst = dq[:, b:b + w].bitcast(dt.uint8) if codes else ds[:, b:b + w]
-            tr.append(RemoteDMATransfer(dst_ids=[DstId(rid=rid, pnc=pid)], dma_engine_mask=mask, remote_sem=sem, src=src, dst=dst))
+            tr.append(transfer(topo, core, d, mask, sems[on_chip(topo, d, core)], src, dst))
             total += len(bits(mask))
         g.remote_dma_fused(tr, local_sem=T.sem.sent)
     return total
@@ -159,6 +195,17 @@ def signs(g, T, which, bank, n0, n1, t0, c, tile, sem):
             g.scalar.activation(out, z, ActivationFunctionType.Relu, scale=sg * c).then_inc(sem, 1)
 
 
+def half_signs(T, eng, k, i, ready, done):
+    z = T.ps[:, 512 * (2 * i + k):512 * (2 * i + k) + 128]
+    eng.wait_ge(ready, 1)
+    for b, sg in enumerate((1.0, -1.0)):
+        out = T.ht[:, 512 * k + 2 * i + b:512 * k + 512:4]
+        if k == 0:
+            eng.tensor_scalar(out, z, sg * C1, 0.0, AluOpType.mult, AluOpType.max).then_inc(done, 1)
+        else:
+            eng.activation(out, z, ActivationFunctionType.Relu, scale=sg * C1).then_inc(done, 1)
+
+
 def product(g, T, banks, wq, ws, q, s, b0, n, sems):
     for i in (0, 1):
         g.tensor.matmul_mx(T.ps[:, 512 * banks[i]:512 * banks[i] + n], wq[:, 128 * i:128 * i + 128], ws[:, 128 * i:128 * i + 128],
@@ -171,92 +218,126 @@ def rank_program(g, core, T, topo):
         P["todo"], P["rise"] = {}, {}
         for c in sorted(set(P["outs"]) | set(P["back"])):
             load = [0.0] * 16
-            for k in ("outs", "back"):
-                P["todo"][c, k] = calls(c, P[k].get(c, []), topo, load, T.cores)
+            for k in ("outs", True, False):
+                todo = P["outs"].get(c, []) if k == "outs" else [r for r in P["back"].get(c, []) if on_chip(topo, r[0], c) == k]
+                P["todo"][c, k] = calls(c, todo, topo, load, T.cores)
                 for _, call in P["todo"][c, k]:
                     for r, mask in call:
-                        P["rise"][r[0], k] = P["rise"].get((r[0], k), 0) + len(bits(mask))
+                        to = (r[0], on_chip(topo, r[0], c) if k == "outs" else "back")
+                        P["rise"][to] = P["rise"].get(to, 0) + len(bits(mask))
         _CACHE["plan"] = P
     P = _CACHE["plan"]
     rank = T.rank_of(core)
     if rank is None and core not in P["role"]:
         return
     S = T.sem
-    a = P["land"][core]
-    tok = P["rise"][core, "outs"]
-    gn = P["gn"][core]
-    own = P["cnt"][rank][rank] if rank is not None else 0
-    sent = 0
-    padded = gn > own + a
-    if padded:
-        g.vector.memset(T.gt[:, 4 * (own + a):4 * gn], 0.0).then_inc(S.pad, 1)
+    group = P["group"][core]
+    pads = 0
+    for near, own, p0, p1, t0, tn in group:
+        k = own + p1 - p0
+        if k < tn:
+            g.vector.memset(T.gt[:, 4 * (t0 + k):4 * (t0 + tn)], 0.0).then_inc(S.pad, 1)
+            pads += 1
+    if pads:
+        g.vector.wait_ge(S.pad, pads)
 
-    def expert(wq, ws, nb, full):
-        g.tensor.wait_ge(S.tok, tok)
-        product(g, T, (4, 5), wq, ws, T.bq, T.bs, NC + a - nb, nb, (S.u0, S.u1))
-        g.vector.wait_ge(S.u0, 1)
-        signs(g, T, 0, 4, nb - a, nb, own, C2, T.gt, S.bv)
-        g.scalar.wait_ge(S.u1, 1)
-        signs(g, T, 1, 5, nb - a, nb, own, C2, T.gt, S.bw)
-        if padded:
-            g.vector.wait_ge(S.pad, 1)
-        g.vector.wait_ge(S.bv, full)
-        g.vector.wait_ge(S.bw, full)
-        g.vector.quantize_mx(T.gq[:, 0:gn], T.gs[:, 0:gn], T.gt[:, 0:4 * gn]).then_inc(S.qg, 1)
-        g.wait_ge(S.qg, 1)
-        k = send(g, T, topo, core, P["todo"][core, "back"], T.gq, T.gs, T.aq, T.as_, S.ret)
-        g.wait_ge(S.sent, sent + k)
+    def expert(wq, ws, full, spare, sent):
+        first = [near for near, _, p0, p1, _, _ in group if p1 > p0][0]
+        for near, own, p0, p1, t0, tn in group:
+            v, w, u0, u1, q, banks = (S.bv, S.bw, S.u0, S.u1, S.qg, (4, 5)) if near else (S.fv, S.fw, S.v0, S.v1, S.qf, (6, 7))
+            k = p1 - p0
+            if k:
+                nb = max(128, k) + (spare if near == first else 0)
+                g.tensor.wait_ge(S.tokn if near else S.tokf, P["rise"][core, near])
+                product(g, T, banks, wq, ws, T.bq, T.bs, NC + p1 - nb, nb, (u0, u1))
+                g.vector.wait_ge(u0, 1)
+                signs(g, T, 0, banks[0], nb - k, nb, t0 + own, C2, T.gt, v)
+                g.scalar.wait_ge(u1, 1)
+                signs(g, T, 1, banks[1], nb - k, nb, t0 + own, C2, T.gt, w)
+            n2 = (2 if k else 0) + (full if near else 0)
+            g.vector.wait_ge(v, n2)
+            g.vector.wait_ge(w, n2)
+            g.vector.quantize_mx(T.gq[:, t0:t0 + tn], T.gs[:, t0:t0 + tn], T.gt[:, 4 * t0:4 * (t0 + tn)]).then_inc(q, 1)
+            if k:
+                g.wait_ge(q, 1)
+                sent += send(g, T, topo, core, P["todo"][core, near], T.gq, T.gs, T.aq, T.as_, (S.ret, S.ret))
+        g.wait_ge(S.sent, sent)
 
     if rank is None:
-        g.tensor.wait_ge(S.w2in, 2 * len(bits(topo.mask(T.cores[P["role"][core]], core))))
-        expert(T.bq, T.bs, max(128, a), 2)
+        f = P["fwdof"][core]
+        tw = P["twin"][f]
+        rid, pid = topo.addr(tw, core)
+        m = topo.mask(core, tw)
+        g.wait_ge(S.fin, len(bits(near_mask(topo, T, f, core))))
+        g.remote_dma(T.bq[:, FC:NC].bitcast(dt.uint8), T.fq[:, FC:NC].bitcast(dt.uint8), S.w2in, S.sent, pid, rid, m)
+        e = P["role"][core]
+        g.tensor.wait_ge(S.w2in, 3 * len(bits(topo.mask(T.cores[e], core))) + len(bits(topo.mask(P["fwd"][e], core))))
+        expert(T.bq, T.bs, 0, 0, len(bits(m)))
         return
 
+    own = P["cnt"][rank][rank]
     off = P["off"][rank]
     o0 = off[rank]
     asl = P["asl"][rank]
     ret = P["rise"][core, "back"]
 
-    g.sync.dma_start(T.xt[:], T.x[:]).then_inc(S.lx, 16)
-    g.scalar.dma_start(T.w1t[:], T.w1[:]).then_inc(S.lw1, 16)
-    g.sync.dma_start(T.w2t[:], T.w2[:]).then_inc(S.lw2, 16)
+    g.sync.dma_start(T.w2t[:, 4 * HW:], T.w2[:, 4 * HW:]).then_inc(S.lw2b, 16)
+    g.scalar.dma_start(T.xt[:], T.x[:]).then_inc(S.lx, 16)
+    g.sync.dma_start(T.w1t[:, 0:512], T.w1[:, 0:512]).then_inc(S.lw1, 16)
+    g.scalar.dma_start(T.w1t[:, 512:1024], T.w1[:, 512:1024]).then_inc(S.lw1b, 16)
+    g.sync.dma_start(T.w2t[:, 0:4 * HW], T.w2[:, 0:4 * HW]).then_inc(S.lw2, 16)
     g.scalar.dma_start(T.w3t[:], T.w3[:]).then_inc(S.lw3, 16)
+
+    g.vector.wait_ge(S.lw2b, 16)
+    g.vector.quantize_mx(T.w2q[:, HW:NC], T.w2s[:, HW:NC], T.w2t[:, 4 * HW:]).then_inc(S.qw2b, 1)
 
     g.vector.wait_ge(S.lx, 16)
     g.vector.quantize_mx(T.xq[:], T.xs[:], T.xt[:]).then_inc(S.qx, 1)
     g.vector.wait_ge(S.lw1, 16)
-    g.vector.quantize_mx(T.w1q[:], T.w1s[:], T.w1t[:]).then_inc(S.qw1, 1)
+    g.vector.quantize_mx(T.w1q[:, 0:128], T.w1s[:, 0:128], T.w1t[:, 0:512]).then_inc(S.qw1, 1)
+    g.vector.wait_ge(S.lw1b, 16)
+    g.vector.quantize_mx(T.w1q[:, 128:NC], T.w1s[:, 128:NC], T.w1t[:, 512:1024]).then_inc(S.qw1b, 1)
+    half_signs(T, g.vector, 0, 0, S.z0, S.av)
+    half_signs(T, g.vector, 0, 1, S.z1, S.av)
+    half_signs(T, g.scalar, 1, 0, S.z2, S.aw)
+    half_signs(T, g.scalar, 1, 1, S.z3, S.aw)
     g.tensor.wait_ge(S.qx, 1)
-    g.tensor.wait_ge(S.qw1, 1)
-    product(g, T, (0, 1), T.w1q, T.w1s, T.xq, T.xs, 0, NC, (S.z0, S.z1))
-    g.vector.wait_ge(S.z0, 1)
-    signs(g, T, 0, 0, 0, NC, 0, C1, T.ht, S.av)
-    g.scalar.wait_ge(S.z1, 1)
-    signs(g, T, 1, 1, 0, NC, 0, C1, T.ht, S.aw)
+    for i, q in ((0, S.qw1), (1, S.qw1b)):
+        g.tensor.wait_ge(q, 1)
+        for k, sems in ((0, (S.z0, S.z1)), (1, (S.z2, S.z3))):
+            b = 512 * (2 * i + k)
+            g.tensor.matmul_mx(T.ps[:, b:b + 128], T.w1q[:, 128 * i:128 * i + 128], T.w1s[:, 128 * i:128 * i + 128],
+                               T.xq[:, 128 * k:128 * k + 128], T.xs[:, 128 * k:128 * k + 128], True, True).then_inc(sems[i], 1)
     g.vector.wait_ge(S.lw2, 16)
-    g.vector.quantize_mx(T.w2q[:], T.w2s[:], T.w2t[:]).then_inc(S.qw2, 1)
-    g.vector.wait_ge(S.av, 2)
-    g.vector.wait_ge(S.aw, 2)
+    g.vector.quantize_mx(T.w2q[:, 0:HW], T.w2s[:, 0:HW], T.w2t[:, 0:4 * HW]).then_inc(S.qw2, 1)
+    g.vector.wait_ge(S.av, 4)
+    g.vector.wait_ge(S.aw, 4)
     g.vector.quantize_mx(T.bq[:, 0:NC], T.bs[:, 0:NC], T.ht[:]).then_inc(S.qh, 1)
 
-    tw = P["twin"][rank]
+    tw, fc = P["twin"][rank], P["fwd"][rank]
     rid, pid = topo.addr(tw, core)
     m = topo.mask(core, tw)
+    fm = near_mask(topo, T, rank, fc)
+    g.wait_ge(S.qw2b, 1)
+    g.remote_dma_fused([transfer(topo, core, tw, m, S.w2in, T.w2q[:, HW:FC].bitcast(dt.uint8), T.bq[:, HW:FC].bitcast(dt.uint8)),
+                        transfer(topo, core, fc, fm, S.fin, T.w2q[:, FC:NC].bitcast(dt.uint8), T.fq[:, FC:NC].bitcast(dt.uint8))],
+                       local_sem=S.sent)
     g.wait_ge(S.qw2, 1)
-    g.remote_dma(T.bq[:, 0:NC].bitcast(dt.uint8), T.w2q[:].bitcast(dt.uint8), S.w2in, S.sent, pid, rid, m)
+    g.remote_dma(T.bq[:, 0:HW].bitcast(dt.uint8), T.w2q[:, 0:HW].bitcast(dt.uint8), S.w2in, S.sent, pid, rid, m)
     g.remote_dma(T.bs[:, 0:NC], T.w2s[:], S.w2in, S.sent, pid, rid, m)
-    sent += 2 * len(bits(m))
+    sent = 3 * len(bits(m)) + len(bits(fm))
     g.wait_ge(S.qh, 1)
-    sent += send(g, T, topo, core, P["todo"][core, "outs"], T.bq, T.bs, T.bq, T.bs, S.tok)
+    sent += send(g, T, topo, core, P["todo"][core, "outs"], T.bq, T.bs, T.bq, T.bs, (S.tokf, S.tokn))
 
     half = ((len(asl) - 1) * 3 + 2) // 5
     e_split = asl[half][0]
     n1, ntot = asl[half][1], asl[-1][1]
     na1, na2 = max(128, n1), max(128, ntot - n1)
-    fixed = 2 * NC + (2 * 128 + 128 if own else 0) + na1 + na2
+    done = 2 * NC + (2 * 128 + 128 if own else 0) + na1 + na2 + sum(2 * max(128, p1 - p0) for _, _, p0, p1, _, _ in group if p1 > p0)
     ow = min(o0, NC - 128)
     g.tensor.wait_ge(S.qh, 1)
     g.tensor.wait_ge(S.qw2, 1)
+    g.tensor.wait_ge(S.qw2b, 1)
     if own:
         product(g, T, (2, 3), T.w2q, T.w2s, T.bq, T.bs, ow, 128, (S.o0, S.o1))
         g.vector.wait_ge(S.o0, 1)
@@ -266,19 +347,19 @@ def rank_program(g, core, T, topo):
     g.vector.wait_ge(S.lw3, 16)
     g.vector.quantize_mx(T.w3q[:], T.w3s[:], T.w3t[:]).then_inc(S.qw3, 1)
 
-    expert(T.w2q, T.w2s, max(128, a, (LEAST - fixed + 3) // 4 * 2), 4 if own else 2)
+    expert(T.w2q, T.w2s, 2 if own else 0, max(0, (LEAST - done + 3) // 4 * 2), sent)
 
     g.tensor.wait_ge(S.qw3, 1)
     if own:
         g.tensor.wait_ge(S.qg, 1)
         g.tensor.matmul_mx(T.ps[:, 1024:1024 + 128], T.w3q[:], T.w3s[:], T.gq[:, 0:128], T.gs[:, 0:128], True, True).then_inc(S.yo, 1)
     g.tensor.wait_ge(S.ret, ret)
-    g.tensor.matmul_mx(T.ps[:, 3072:3072 + na1], T.w3q[:], T.w3s[:], T.aq[:, 0:na1], T.as_[:, 0:na1], True, True).then_inc(S.y1, 1)
-    g.tensor.matmul_mx(T.ps[:, 3584:3584 + na2], T.w3q[:], T.w3s[:], T.aq[:, ntot - na2:ntot], T.as_[:, ntot - na2:ntot],
+    g.tensor.matmul_mx(T.ps[:, 0:na1], T.w3q[:], T.w3s[:], T.aq[:, 0:na1], T.as_[:, 0:na1], True, True).then_inc(S.y1, 1)
+    g.tensor.matmul_mx(T.ps[:, 512:512 + na2], T.w3q[:], T.w3s[:], T.aq[:, ntot - na2:ntot], T.as_[:, ntot - na2:ntot],
                        True, True).then_inc(S.y2, 1)
     for part in (0, 1):
         eng, sem, done = (g.vector, S.y1, S.cv) if part == 0 else (g.scalar, S.y2, S.cw)
-        base = 3072 if part == 0 else 3584 - (ntot - na2)
+        base = 0 if part == 0 else 512 - (ntot - na2)
         segs = []
         for e, pos, o, c in (asl[:half] if part == 0 else asl[half:-1]):
             y0, src = off[e], base + pos + o

@@ -5,9 +5,9 @@ NC = 256
 C1, C2 = 0.043, 0.041
 LEAST = 1280
 SIM_CORES = 512
-CABLE_TWIN = (0, 3, 4, 6, 8, 10, 13, 14)
+CABLE_TWIN = (1, 3, 5, 6, 8, 11, 12, 15)
 HW, FC = 128, 192
-ALPHA = 45
+ALPHA = 8
 
 CODES, PLANE = "float8_e4m3fn_x4", "uint8"
 SCRATCH = {
@@ -22,7 +22,7 @@ SCRATCH = {
     "w1q": ("sbuf", [128, 256], CODES), "w1s": ("sbuf", [128, 256], PLANE),
     "w2q": ("sbuf", [128, 256], CODES), "w2s": ("sbuf", [128, 256], PLANE),
     "w3q": ("sbuf", [128, 128], CODES), "w3s": ("sbuf", [128, 128], PLANE),
-    "fq": ("sbuf", [128, 256], CODES),
+    "fq": ("sbuf", [128, 256], CODES), "fs": ("sbuf", [128, 256], PLANE),
     "bq": ("sbuf", [128, 768], CODES), "bs": ("sbuf", [128, 768], PLANE),
     "gq": ("sbuf", [128, 512], CODES), "gs": ("sbuf", [128, 512], PLANE),
     "aq": ("sbuf", [128, 768], CODES), "as_": ("sbuf", [128, 768], PLANE),
@@ -30,7 +30,7 @@ SCRATCH = {
 }
 SEMAPHORES = ["lx", "lw1", "lw1b", "lw2", "lw2b", "lw3", "qx", "qw1", "qw1b", "qw2", "qw2b", "qw3", "qh", "qg", "qf",
               "z0", "z1", "z2", "z3", "o0", "o1", "u0", "u1", "v0", "v1", "av", "aw", "bv", "bw", "fv", "fw", "pad", "sent",
-              "w2in", "fin", "tokn", "tokf", "ret", "yo", "y1", "y2", "cv", "cw", "st1", "st2"]
+              "w2in", "fin", "fin2", "tokn", "tokf", "ret", "yo", "y1", "y2", "cv", "cw", "st1", "st2"]
 _CACHE = {}
 
 
@@ -268,11 +268,14 @@ def rank_program(g, core, T, topo):
         tw = P["twin"][f]
         rid, pid = topo.addr(tw, core)
         m = topo.mask(core, tw)
-        g.wait_ge(S.fin, len(bits(near_mask(topo, T, f, core))))
-        g.remote_dma(T.bq[:, FC:NC].bitcast(dt.uint8), T.fq[:, FC:NC].bitcast(dt.uint8), S.w2in, S.sent, pid, rid, m)
+        nf = len(bits(near_mask(topo, T, f, core)))
+        g.wait_ge(S.fin, nf)
+        g.remote_dma(T.bq[:, HW:FC].bitcast(dt.uint8), T.fq[:, HW:FC].bitcast(dt.uint8), S.w2in, S.sent, pid, rid, m)
+        g.wait_ge(S.fin2, nf)
+        g.remote_dma(T.bs[:, 0:NC], T.fs[:], S.w2in, S.sent, pid, rid, m)
         e = P["role"][core]
-        g.tensor.wait_ge(S.w2in, 3 * len(bits(topo.mask(T.cores[e], core))) + len(bits(topo.mask(P["fwd"][e], core))))
-        expert(T.bq, T.bs, 0, 0, len(bits(m)))
+        g.tensor.wait_ge(S.w2in, 2 * len(bits(topo.mask(T.cores[e], core))) + 2 * len(bits(topo.mask(P["fwd"][e], core))))
+        expert(T.bq, T.bs, 0, 0, 2 * len(bits(m)))
         return
 
     own = P["cnt"][rank][rank]
@@ -316,16 +319,17 @@ def rank_program(g, core, T, topo):
 
     tw, fc = P["twin"][rank], P["fwd"][rank]
     rid, pid = topo.addr(tw, core)
+    frid, fpid = topo.addr(fc, core)
     m = topo.mask(core, tw)
     fm = near_mask(topo, T, rank, fc)
     g.wait_ge(S.qw2b, 1)
-    g.remote_dma_fused([transfer(topo, core, tw, m, S.w2in, T.w2q[:, HW:FC].bitcast(dt.uint8), T.bq[:, HW:FC].bitcast(dt.uint8)),
-                        transfer(topo, core, fc, fm, S.fin, T.w2q[:, FC:NC].bitcast(dt.uint8), T.fq[:, FC:NC].bitcast(dt.uint8))],
+    g.remote_dma_fused([transfer(topo, core, tw, m, S.w2in, T.w2q[:, FC:NC].bitcast(dt.uint8), T.bq[:, FC:NC].bitcast(dt.uint8)),
+                        transfer(topo, core, fc, fm, S.fin, T.w2q[:, HW:FC].bitcast(dt.uint8), T.fq[:, HW:FC].bitcast(dt.uint8))],
                        local_sem=S.sent)
     g.wait_ge(S.qw2, 1)
     g.remote_dma(T.bq[:, 0:HW].bitcast(dt.uint8), T.w2q[:, 0:HW].bitcast(dt.uint8), S.w2in, S.sent, pid, rid, m)
-    g.remote_dma(T.bs[:, 0:NC], T.w2s[:], S.w2in, S.sent, pid, rid, m)
-    sent = 3 * len(bits(m)) + len(bits(fm))
+    g.remote_dma(T.fs[:], T.w2s[:], S.fin2, S.sent, fpid, frid, fm)
+    sent = 2 * len(bits(m)) + 2 * len(bits(fm))
     g.wait_ge(S.qh, 1)
     sent += send(g, T, topo, core, P["todo"][core, "outs"], T.bq, T.bs, T.bq, T.bs, (S.tokf, S.tokn))
 

from concourse.bass import DstId, RemoteDMATransfer
from concourse.mybir import dt, AluOpType, ActivationFunctionType

NC = 256
C1, C2 = 0.043, 0.041
LEAST = 1280
SIM_CORES = 512
CABLE_TWIN = (1, 3, 5, 6, 8, 11, 12, 15)
HW, FC = 128, 192
ALPHA = 8

CODES, PLANE = "float8_e4m3fn_x4", "uint8"
SCRATCH = {
    "xt": ("sbuf", [128, 1024], "bfloat16"),
    "w1t": ("sbuf", [128, 1024], "bfloat16"),
    "w2t": ("sbuf", [128, 1024], "bfloat16"),
    "w3t": ("sbuf", [128, 512], "bfloat16"),
    "ht": ("sbuf", [128, 1024], "bfloat16"),
    "gt": ("sbuf", [128, 2048], "bfloat16"),
    "ysb": ("sbuf", [128, 256], "float32"),
    "xq": ("sbuf", [128, 256], CODES), "xs": ("sbuf", [128, 256], PLANE),
    "w1q": ("sbuf", [128, 256], CODES), "w1s": ("sbuf", [128, 256], PLANE),
    "w2q": ("sbuf", [128, 256], CODES), "w2s": ("sbuf", [128, 256], PLANE),
    "w3q": ("sbuf", [128, 128], CODES), "w3s": ("sbuf", [128, 128], PLANE),
    "fq": ("sbuf", [128, 256], CODES), "fs": ("sbuf", [128, 256], PLANE),
    "bq": ("sbuf", [128, 768], CODES), "bs": ("sbuf", [128, 768], PLANE),
    "gq": ("sbuf", [128, 512], CODES), "gs": ("sbuf", [128, 512], PLANE),
    "aq": ("sbuf", [128, 768], CODES), "as_": ("sbuf", [128, 768], PLANE),
    "ps": ("psum", [128, 4096], "float32"),
}
SEMAPHORES = ["lx", "lw1", "lw1b", "lw2", "lw2b", "lw3", "qx", "qw1", "qw1b", "qw2", "qw2b", "qw3", "qh", "qg", "qf",
              "z0", "z1", "z2", "z3", "o0", "o1", "u0", "u1", "v0", "v1", "av", "aw", "bv", "bw", "fv", "fw", "pad", "sent",
              "w2in", "fin", "fin2", "tokn", "tokf", "ret", "yo", "y1", "y2", "cv", "cw", "st1", "st2"]
_CACHE = {}


def widths(counts):
    ds = sorted(set(counts))
    best = None
    for m in range(1 << (len(ds) - 1)):
        ws = [d for i, d in enumerate(ds[:-1]) if m >> i & 1] + [ds[-1]]
        cost = 2 * ALPHA * len(ws) + sum(min(w for w in ws if w >= c) - c for c in counts)
        if best is None or cost < best[0]:
            best = (cost, ws)
    return best[1]


def on_chip(topo, a, b):
    return topo.chip(a) == topo.chip(b) and topo.host(a) == topo.host(b)


def make_plan(T, topo):
    cnt, cores = T.tables["CNT"], list(T.cores)
    n = len(cores)
    off = [[sum(c[:e]) for e in range(n + 1)] for c in cnt]
    host = [topo.host(c) for c in cores]

    def spare(h, e):
        return [c for c in range(SIM_CORES) if topo.host(c) == h and topo.chip(c) == topo.chip(cores[e]) and T.rank_of(c) is None]

    twin, used, role = {}, {}, {}
    for cabled in (False, True):
        for e in range(n):
            if (e in CABLE_TWIN) != cabled:
                continue
            th = [h for h in sorted(set(host)) if h != host[e] and topo.may_write(cores[e], cores[host.index(h)])
                  and (topo.rack(h) != topo.rack(host[e])) == cabled][0]
            k = used.get((th, cabled), 0)
            used[(th, cabled)] = k + 1
            twin[e] = spare(th, e)[2 * k + int(cabled)]
            role[twin[e]] = e
    fwd, fwdof = {}, {}
    for e in range(n):
        k = [f for f in range(n) if host[f] == host[e] and (f in CABLE_TWIN) == (e in CABLE_TWIN)].index(e)
        fwd[e] = spare(host[e], e)[2 * k + int(e in CABLE_TWIN)]
        fwdof[fwd[e]] = e

    def site(j, e):
        if host[j] != topo.host(twin[e]) and topo.may_write(cores[j], cores[e]):
            return cores[e]
        return twin[e]
    runs, outs = {}, {}
    for j in range(n):
        items = [(e, cnt[j][e]) for e in range(n) if e != j and cnt[j][e]]
        ws = widths([c for _, c in items])
        for e, c in items:
            w = min(v for v in ws if v >= c)
            s = min(off[j][e], NC - w)
            d = site(j, e)
            runs.setdefault(d, {True: [], False: []})[on_chip(topo, cores[j], d)].append((j, w, s, off[j][e] - s, c))
    back, pieces, group = {}, {}, {}
    for d in sorted(runs):
        e = role[d] if d in role else T.rank_of(d)
        p, t0 = 0, 0
        group[d] = []
        for near in (True, False):
            own = cnt[e][e] if d not in role and near else 0
            p0 = p
            ws = widths([r[4] for r in runs[d][near]]) if runs[d][near] else []
            tn = max(128, own + sum(r[1] for r in runs[d][near]))
            for j, w, s, o, c in runs[d][near]:
                outs.setdefault(cores[j], []).append((d, s, NC + p, w))
                v = min(v for v in ws if v >= c)
                col = own + p - p0 + o
                src = min(col, tn - v)
                pieces.setdefault(j, []).append((e, d, v, col - src, c, t0 + src))
                p += w
            if own or p > p0:
                group[d].append((near, own, p0, p, t0, tn))
                t0 += tn
    for c in outs:
        outs[c].sort(key=lambda r: r[1])
    asl = {}
    for j in range(n):
        pos = 0
        asl[j] = []
        for e, s, w, o, c, src in sorted(pieces[j]):
            asl[j].append((e, pos, o, c))
            back.setdefault(s, []).append((cores[j], src, pos, w))
            pos += w
        asl[j].append((n, pos, 0, 0))
    return {"cnt": cnt, "off": off, "twin": twin, "role": role, "outs": outs, "back": back, "asl": asl, "group": group,
            "fwd": fwd, "fwdof": fwdof}


def bits(mask):
    return [b for b in range(16) if mask >> b & 1]


def calls(core, runs, topo, load, ends):
    out = []
    outside = 0
    for c in ends:
        if topo.host(c) != topo.host(core) and topo.may_write(core, c):
            outside = outside | topo.mask(core, c)
    for w in sorted(set(r[3] for r in runs), reverse=True):
        group = [r for r in runs if r[3] == w]
        far = [r for r in group if not on_chip(topo, r[0], core)]
        near = [r for r in group if r not in far]
        for codes in (True, False):
            call = []
            for part in (far, near):
                if not part:
                    continue
                pool = bits(outside) if part is far else [b for b in bits(topo.mask(core, part[0][0])) if not far or not outside >> b & 1]
                p = 1
                while 2 * p * len(part) <= len(pool):
                    p *= 2
                extra = (len(pool) - p * len(part)) // p
                pool = sorted(pool, key=lambda b: (load[b], b))
                for i, r in enumerate(part):
                    k = p if i < len(part) - extra else 2 * p
                    es, pool = pool[:k], pool[k:]
                    call.append((r, sum(1 << b for b in es)))
                    for b in es:
                        load[b] += (40 + (4 * w if codes else w) / 12.0) / k
            out.append((codes, call))
    return out


def near_mask(topo, T, e, c):
    out = 0
    for t in T.cores:
        if topo.host(t) != topo.host(T.cores[e]) and topo.may_write(T.cores[e], t):
            out = out | topo.mask(T.cores[e], t)
    return topo.mask(T.cores[e], c) & ~out


def transfer(topo, core, dst, mask, sem, src, to):
    rid, pid = topo.addr(dst, core)
    return RemoteDMATransfer(dst_ids=[DstId(rid=rid, pnc=pid)], dma_engine_mask=mask, remote_sem=sem, src=src, dst=to)


def send(g, T, topo, core, todo, q, s, dq, ds, sems):
    total = 0
    for codes, call in todo:
        tr = []
        for (d, a, b, w), mask in call:
            src = q[:, a:a + w].bitcast(dt.uint8) if codes else s[:, a:a + w]
            dst = dq[:, b:b + w].bitcast(dt.uint8) if codes else ds[:, b:b + w]
            tr.append(transfer(topo, core, d, mask, sems[on_chip(topo, d, core)], src, dst))
            total += len(bits(mask))
        g.remote_dma_fused(tr, local_sem=T.sem.sent)
    return total


def signs(g, T, which, bank, n0, n1, t0, c, tile, sem):
    z = T.ps[:, 512 * bank + n0:512 * bank + n1]
    e = t0 + n1 - n0
    for k, sg in enumerate((1.0, -1.0)):
        out = tile[:, 4 * t0 + 2 * which + k:4 * e:4]
        if which == 0:
            g.vector.tensor_scalar(out, z, sg * c, 0.0, AluOpType.mult, AluOpType.max).then_inc(sem, 1)
        else:
            g.scalar.activation(out, z, ActivationFunctionType.Relu, scale=sg * c).then_inc(sem, 1)


def half_signs(T, eng, k, i, ready, done):
    z = T.ps[:, 512 * (2 * i + k):512 * (2 * i + k) + 128]
    eng.wait_ge(ready, 1)
    for b, sg in enumerate((1.0, -1.0)):
        out = T.ht[:, 512 * k + 2 * i + b:512 * k + 512:4]
        if k == 0:
            eng.tensor_scalar(out, z, sg * C1, 0.0, AluOpType.mult, AluOpType.max).then_inc(done, 1)
        else:
            eng.activation(out, z, ActivationFunctionType.Relu, scale=sg * C1).then_inc(done, 1)


def product(g, T, banks, wq, ws, q, s, b0, n, sems):
    for i in (0, 1):
        g.tensor.matmul_mx(T.ps[:, 512 * banks[i]:512 * banks[i] + n], wq[:, 128 * i:128 * i + 128], ws[:, 128 * i:128 * i + 128],
                           q[:, b0:b0 + n], s[:, b0:b0 + n], True, True).then_inc(sems[i], 1)


def rank_program(g, core, T, topo):
    if "plan" not in _CACHE:
        P = make_plan(T, topo)
        P["todo"], P["rise"] = {}, {}
        for c in sorted(set(P["outs"]) | set(P["back"])):
            load = [0.0] * 16
            for k in ("outs", True, False):
                todo = P["outs"].get(c, []) if k == "outs" else [r for r in P["back"].get(c, []) if on_chip(topo, r[0], c) == k]
                P["todo"][c, k] = calls(c, todo, topo, load, T.cores)
                for _, call in P["todo"][c, k]:
                    for r, mask in call:
                        to = (r[0], on_chip(topo, r[0], c) if k == "outs" else "back")
                        P["rise"][to] = P["rise"].get(to, 0) + len(bits(mask))
        _CACHE["plan"] = P
    P = _CACHE["plan"]
    rank = T.rank_of(core)
    if rank is None and core not in P["role"]:
        return
    S = T.sem
    group = P["group"][core]
    pads = 0
    for near, own, p0, p1, t0, tn in group:
        k = own + p1 - p0
        if k < tn:
            g.vector.memset(T.gt[:, 4 * (t0 + k):4 * (t0 + tn)], 0.0).then_inc(S.pad, 1)
            pads += 1
    if pads:
        g.vector.wait_ge(S.pad, pads)

    def expert(wq, ws, full, spare, sent):
        first = [near for near, _, p0, p1, _, _ in group if p1 > p0][0]
        for near, own, p0, p1, t0, tn in group:
            v, w, u0, u1, q, banks = (S.bv, S.bw, S.u0, S.u1, S.qg, (4, 5)) if near else (S.fv, S.fw, S.v0, S.v1, S.qf, (6, 7))
            k = p1 - p0
            if k:
                nb = max(128, k) + (spare if near == first else 0)
                g.tensor.wait_ge(S.tokn if near else S.tokf, P["rise"][core, near])
                product(g, T, banks, wq, ws, T.bq, T.bs, NC + p1 - nb, nb, (u0, u1))
                g.vector.wait_ge(u0, 1)
                signs(g, T, 0, banks[0], nb - k, nb, t0 + own, C2, T.gt, v)
                g.scalar.wait_ge(u1, 1)
                signs(g, T, 1, banks[1], nb - k, nb, t0 + own, C2, T.gt, w)
            n2 = (2 if k else 0) + (full if near else 0)
            g.vector.wait_ge(v, n2)
            g.vector.wait_ge(w, n2)
            g.vector.quantize_mx(T.gq[:, t0:t0 + tn], T.gs[:, t0:t0 + tn], T.gt[:, 4 * t0:4 * (t0 + tn)]).then_inc(q, 1)
            if k:
                g.wait_ge(q, 1)
                sent += send(g, T, topo, core, P["todo"][core, near], T.gq, T.gs, T.aq, T.as_, (S.ret, S.ret))
        g.wait_ge(S.sent, sent)

    if rank is None:
        f = P["fwdof"][core]
        tw = P["twin"][f]
        rid, pid = topo.addr(tw, core)
        m = topo.mask(core, tw)
        nf = len(bits(near_mask(topo, T, f, core)))
        g.wait_ge(S.fin, nf)
        g.remote_dma(T.bq[:, HW:FC].bitcast(dt.uint8), T.fq[:, HW:FC].bitcast(dt.uint8), S.w2in, S.sent, pid, rid, m)
        g.wait_ge(S.fin2, nf)
        g.remote_dma(T.bs[:, 0:NC], T.fs[:], S.w2in, S.sent, pid, rid, m)
        e = P["role"][core]
        g.tensor.wait_ge(S.w2in, 2 * len(bits(topo.mask(T.cores[e], core))) + 2 * len(bits(topo.mask(P["fwd"][e], core))))
        expert(T.bq, T.bs, 0, 0, 2 * len(bits(m)))
        return

    own = P["cnt"][rank][rank]
    off = P["off"][rank]
    o0 = off[rank]
    asl = P["asl"][rank]
    ret = P["rise"][core, "back"]

    g.sync.dma_start(T.w2t[:, 4 * HW:], T.w2[:, 4 * HW:]).then_inc(S.lw2b, 16)
    g.scalar.dma_start(T.xt[:], T.x[:]).then_inc(S.lx, 16)
    g.sync.dma_start(T.w1t[:, 0:512], T.w1[:, 0:512]).then_inc(S.lw1, 16)
    g.scalar.dma_start(T.w1t[:, 512:1024], T.w1[:, 512:1024]).then_inc(S.lw1b, 16)
    g.sync.dma_start(T.w2t[:, 0:4 * HW], T.w2[:, 0:4 * HW]).then_inc(S.lw2, 16)
    g.scalar.dma_start(T.w3t[:], T.w3[:]).then_inc(S.lw3, 16)

    g.vector.wait_ge(S.lw2b, 16)
    g.vector.quantize_mx(T.w2q[:, HW:NC], T.w2s[:, HW:NC], T.w2t[:, 4 * HW:]).then_inc(S.qw2b, 1)

    g.vector.wait_ge(S.lx, 16)
    g.vector.quantize_mx(T.xq[:], T.xs[:], T.xt[:]).then_inc(S.qx, 1)
    g.vector.wait_ge(S.lw1, 16)
    g.vector.quantize_mx(T.w1q[:, 0:128], T.w1s[:, 0:128], T.w1t[:, 0:512]).then_inc(S.qw1, 1)
    g.vector.wait_ge(S.lw1b, 16)
    g.vector.quantize_mx(T.w1q[:, 128:NC], T.w1s[:, 128:NC], T.w1t[:, 512:1024]).then_inc(S.qw1b, 1)
    half_signs(T, g.vector, 0, 0, S.z0, S.av)
    half_signs(T, g.vector, 0, 1, S.z1, S.av)
    half_signs(T, g.scalar, 1, 0, S.z2, S.aw)
    half_signs(T, g.scalar, 1, 1, S.z3, S.aw)
    g.tensor.wait_ge(S.qx, 1)
    for i, q in ((0, S.qw1), (1, S.qw1b)):
        g.tensor.wait_ge(q, 1)
        for k, sems in ((0, (S.z0, S.z1)), (1, (S.z2, S.z3))):
            b = 512 * (2 * i + k)
            g.tensor.matmul_mx(T.ps[:, b:b + 128], T.w1q[:, 128 * i:128 * i + 128], T.w1s[:, 128 * i:128 * i + 128],
                               T.xq[:, 128 * k:128 * k + 128], T.xs[:, 128 * k:128 * k + 128], True, True).then_inc(sems[i], 1)
    g.vector.wait_ge(S.lw2, 16)
    g.vector.quantize_mx(T.w2q[:, 0:HW], T.w2s[:, 0:HW], T.w2t[:, 0:4 * HW]).then_inc(S.qw2, 1)
    g.vector.wait_ge(S.av, 4)
    g.vector.wait_ge(S.aw, 4)
    g.vector.quantize_mx(T.bq[:, 0:NC], T.bs[:, 0:NC], T.ht[:]).then_inc(S.qh, 1)

    tw, fc = P["twin"][rank], P["fwd"][rank]
    rid, pid = topo.addr(tw, core)
    frid, fpid = topo.addr(fc, core)
    m = topo.mask(core, tw)
    fm = near_mask(topo, T, rank, fc)
    g.wait_ge(S.qw2b, 1)
    g.remote_dma_fused([transfer(topo, core, tw, m, S.w2in, T.w2q[:, FC:NC].bitcast(dt.uint8), T.bq[:, FC:NC].bitcast(dt.uint8)),
                        transfer(topo, core, fc, fm, S.fin, T.w2q[:, HW:FC].bitcast(dt.uint8), T.fq[:, HW:FC].bitcast(dt.uint8))],
                       local_sem=S.sent)
    g.wait_ge(S.qw2, 1)
    g.remote_dma(T.bq[:, 0:HW].bitcast(dt.uint8), T.w2q[:, 0:HW].bitcast(dt.uint8), S.w2in, S.sent, pid, rid, m)
    g.remote_dma(T.fs[:], T.w2s[:], S.fin2, S.sent, fpid, frid, fm)
    sent = 2 * len(bits(m)) + 2 * len(bits(fm))
    g.wait_ge(S.qh, 1)
    sent += send(g, T, topo, core, P["todo"][core, "outs"], T.bq, T.bs, T.bq, T.bs, (S.tokf, S.tokn))

    half = ((len(asl) - 1) * 3 + 2) // 5
    e_split = asl[half][0]
    n1, ntot = asl[half][1], asl[-1][1]
    na1, na2 = max(128, n1), max(128, ntot - n1)
    done = 2 * NC + (2 * 128 + 128 if own else 0) + na1 + na2 + sum(2 * max(128, p1 - p0) for _, _, p0, p1, _, _ in group if p1 > p0)
    ow = min(o0, NC - 128)
    g.tensor.wait_ge(S.qh, 1)
    g.tensor.wait_ge(S.qw2, 1)
    g.tensor.wait_ge(S.qw2b, 1)
    if own:
        product(g, T, (2, 3), T.w2q, T.w2s, T.bq, T.bs, ow, 128, (S.o0, S.o1))
        g.vector.wait_ge(S.o0, 1)
        signs(g, T, 0, 2, o0 - ow, o0 - ow + own, 0, C2, T.gt, S.bv)
        g.scalar.wait_ge(S.o1, 1)
        signs(g, T, 1, 3, o0 - ow, o0 - ow + own, 0, C2, T.gt, S.bw)
    g.vector.wait_ge(S.lw3, 16)
    g.vector.quantize_mx(T.w3q[:], T.w3s[:], T.w3t[:]).then_inc(S.qw3, 1)

    expert(T.w2q, T.w2s, 2 if own else 0, max(0, (LEAST - done + 3) // 4 * 2), sent)

    g.tensor.wait_ge(S.qw3, 1)
    if own:
        g.tensor.wait_ge(S.qg, 1)
        g.tensor.matmul_mx(T.ps[:, 1024:1024 + 128], T.w3q[:], T.w3s[:], T.gq[:, 0:128], T.gs[:, 0:128], True, True).then_inc(S.yo, 1)
    g.tensor.wait_ge(S.ret, ret)
    g.tensor.matmul_mx(T.ps[:, 0:na1], T.w3q[:], T.w3s[:], T.aq[:, 0:na1], T.as_[:, 0:na1], True, True).then_inc(S.y1, 1)
    g.tensor.matmul_mx(T.ps[:, 512:512 + na2], T.w3q[:], T.w3s[:], T.aq[:, ntot - na2:ntot], T.as_[:, ntot - na2:ntot],
                       True, True).then_inc(S.y2, 1)
    for part in (0, 1):
        eng, sem, done = (g.vector, S.y1, S.cv) if part == 0 else (g.scalar, S.y2, S.cw)
        base = 0 if part == 0 else 512 - (ntot - na2)
        segs = []
        for e, pos, o, c in (asl[:half] if part == 0 else asl[half:-1]):
            y0, src = off[e], base + pos + o
            if segs and segs[-1][1] == y0 and segs[-1][2] + segs[-1][1] - segs[-1][0] == src:
                segs[-1][1] = y0 + c
            else:
                segs.append([y0, y0 + c, src])
        mine = own and (rank < e_split) == (part == 0)
        if mine:
            segs.insert(0, [o0, o0 + own, 1024])
        for i, (lo, hi, src) in enumerate(segs):
            if mine and i == 0:
                eng.wait_ge(S.yo, 1)
            if i == (1 if mine else 0):
                eng.wait_ge(sem, 1)
            if part == 0:
                g.vector.tensor_copy(T.ysb[:, lo:hi], T.ps[:, src:src + hi - lo]).then_inc(done, 1)
            else:
                g.scalar.activation(T.ysb[:, lo:hi], T.ps[:, src:src + hi - lo], ActivationFunctionType.Copy).then_inc(done, 1)
        q, st = (g.sync, S.st1) if part == 0 else (g.scalar, S.st2)
        lo, hi = (0, off[e_split]) if part == 0 else (off[e_split], NC)
        q.wait_ge(done, len(segs))
        q.dma_start(T.y[:, lo:hi], T.ysb[:, lo:hi]).then_inc(st, 16)
    g.sync.wait_ge(S.st1, 16)
    g.scalar.wait_ge(S.st2, 16)
